import numpy as np
import ml_dtypes


def mxq(x, axis, fmt="e4m3"):
    dtype, down = {"e4m3": (ml_dtypes.float8_e4m3fn, 7), "e5m2": (ml_dtypes.float8_e5m2, 14)}[fmt]
    v = np.moveaxis(np.asarray(x, np.float32).astype(ml_dtypes.bfloat16).astype(np.float64), axis, -1)
    blocks = v.reshape(v.shape[:-1] + (-1, 32))
    amax = np.abs(blocks).max(-1, keepdims=True)
    byte = np.maximum(np.where(amax > 0, np.frexp(amax)[1] - 1 + 127, 0) - down, 1)
    scale = np.exp2(byte - 127.0)
    codes = (blocks / scale).astype(np.float32).astype(dtype).astype(np.float64)
    return np.moveaxis((codes * scale).reshape(v.shape), -1, axis)


WIDE = False


def mx_kscale(k):
    if not WIDE:
        return np.ones(k)
    levels = np.array([10, -10, 5, -5, 0])
    if k % 512:
        return np.exp2(np.random.permutation(np.resize(levels, k // 32))).repeat(32)
    a = np.empty((k // 512, 16))
    for p in range(k // 512):
        a[p, :8] = np.random.permutation(np.resize(levels, 8))
        for g in range(8):
            far = levels[np.abs(levels - a[p, g]) >= 10]
            a[p, g + 8] = far[np.random.randint(len(far))]
    return np.exp2(a.ravel()).repeat(32)


def f64(x):
    return np.asarray(x).astype(np.float64)


def striped(idx):
    return np.tile(np.asarray(idx).reshape(-1, 16).T, (8, 1)).astype(np.uint16)


def unstriped(offs):
    return offs[:16].T.reshape(-1).astype(np.int64)


E2M1 = np.array([0.0, 0.5, 1.0, 1.5, 2.0, 3.0, 4.0, 6.0, -0.0, -0.5, -1.0, -1.5, -2.0, -3.0, -4.0, -6.0])


def pack_weight(w, fmt):
    k, n = w.shape
    w = f64(np.asarray(w, np.float32).astype(ml_dtypes.bfloat16)).reshape(k // 32, 32, n)
    amax = np.abs(w).max(1)
    if fmt == "e4m3":
        byte = np.frexp(amax)[1] - 1 + 127 - 7
    else:
        mant, ex = np.frexp(amax / 6.0)
        byte = np.where(mant > 0.5, ex, ex - 1) + 127
    byte = np.clip(np.where(amax > 0, byte, 1), 1, 254)
    scaled = (w * np.exp2(127.0 - byte)[:, None, :]).reshape(k, n).astype(np.float32)
    by_word = np.ascontiguousarray(scaled.reshape(k // 512, 128, 4, n).transpose(0, 1, 3, 2))
    if fmt == "e4m3":
        words = by_word.astype(ml_dtypes.float8_e4m3fn).view(np.uint8)
    else:
        c = by_word.astype(ml_dtypes.float4_e2m1fn).view(np.uint8) & 0xF
        words = (c[..., 0::2] | (c[..., 1::2] << 4)).reshape(k // 512, 128, 2 * n)
    return np.ascontiguousarray(words), np.ascontiguousarray(byte.astype(np.uint8).reshape(k // 512, 16, n))


def unpack_weight(words, scales, fmt):
    g, _, n = scales.shape
    words = np.ascontiguousarray(words).reshape(g, 128, n, -1)
    if fmt == "e4m3":
        vals = words.view(ml_dtypes.float8_e4m3fn).astype(np.float64)
    else:
        nib = np.empty((g, 128, n, 4), np.uint8)
        nib[..., 0::2] = words & 0xF
        nib[..., 1::2] = words >> 4
        vals = E2M1[nib]
    vals = vals * np.repeat(np.exp2(scales.astype(np.float64) - 127.0), 8, axis=1)[..., None]
    return vals.transpose(0, 1, 3, 2).reshape(g * 512, n)


def sigmoid(v):
    return 1.0 / (1.0 + np.exp(-v))


D, T, I, Q, E, U, M = 512, 2048, 512, 512, 512, 1024, 1024


def setup_inputs():
    n = np.random.standard_normal
    idx = np.random.permutation(T)[:I]
    idx2 = np.random.permutation(U)[:I]
    idx3 = np.random.permutation(M)[:I]
    fd = mx_kscale(D)
    fq = mx_kscale(Q)
    keysp = pack_weight(n((D, T)) / fd[:, None], "e4m3")
    return {
        "query": (n((D, Q)) * 0.7 / np.sqrt(D) * fd[:, None]).astype(np.float32),
        "query2": (n((D, Q)) * 0.7 / np.sqrt(D) * fd[:, None]).astype(np.float32),
        "keys_words": keysp[0],
        "keys_scales": keysp[1],
        "notes": (n((D, U)) / fd[:, None]).astype(np.float32),
        "qs": (np.random.uniform(0.5, 2.0, (Q, 1)) * fq[:, None]).astype(np.float32),
        "msgs": (n((Q, E)) * 1 / np.sqrt(Q) / fq[:, None]).astype(np.float32),
        "old": (n((E, M)) * 1.0).astype(np.float32),
        "fade": (np.random.uniform(0.3, 0.9, (1, M))).astype(np.float32),
        "offs": striped(idx),
        "offs2": striped(idx2),
        "offs3": striped(idx3),
    }


def reference(query, query2, keys_words, keys_scales, notes, qs, msgs, old, fade, offs, offs2, offs3):
    idx = unstriped(offs)
    idx2 = unstriped(offs2)
    idx3 = unstriped(offs3)
    keysu = unpack_weight(keys_words, keys_scales, "e4m3")
    queryq = mxq(f64(query), 0, "e4m3")
    keysidxg = keysu[:, idx]
    query2q = mxq(f64(query2), 0, "e4m3")
    notesidx2q = mxq(f64(notes)[:, idx2], 0, "e4m3")
    s = queryq.T @ keysidxg + query2q.T @ notesidx2q
    w = sigmoid(s)
    wq = w * f64(qs)
    msgsq = mxq(f64(msgs), 0, "e4m3")
    wqq = mxq(wq, 0, "e4m3")
    dl = msgsq.T @ wqq
    df = np.zeros((E, M))
    df[:, idx3] = dl
    y = f64(old) * f64(fade) + df
    return y

@@ -1,0 +1,229 @@
+from contextlib import ExitStack
+
+import concourse.mybir as mybir
+from concourse.masks import make_identity
+
+D, T, I, Q, E, U, M = 512, 2048, 512, 512, 512, 1024, 1024
+FLOPS = 2 * Q * I * D * 2 + 2 * E * I * Q
+
+F32 = mybir.dt.float32
+BF16 = mybir.dt.bfloat16
+I32 = mybir.dt.int32
+U32 = mybir.dt.uint32
+U16 = mybir.dt.uint16
+U8 = mybir.dt.uint8
+FP8X4 = mybir.dt.float8_e4m3fn_x4
+MULT = mybir.AluOpType.mult
+ADD = mybir.AluOpType.add
+COPY = mybir.ActivationFunctionType.Copy
+SIGMOID = mybir.ActivationFunctionType.Sigmoid
+
+P = 128
+PACK = 4
+CHUNK = 128
+CHUNKS = I // CHUNK
+PER_COL = 16
+BANK = 512
+
+
+def tile_attend_twosources_delivered_lean_kernel(
+    tc, query, query2, keys_words, keys_scales, notes, qs, msgs, old, fade, offs, offs2, offs3, out
+):
+    nc = tc.nc
+    with ExitStack() as ctx:
+        lists = ctx.enter_context(tc.tile_pool(name="lists", bufs=1))
+        sb = ctx.enter_context(tc.tile_pool(name="sb", bufs=1))
+        ps_fade = ctx.enter_context(tc.psum_pool(name="ps_fade", bufs=1))
+        ps = ctx.enter_context(tc.psum_pool(name="ps", bufs=6))
+
+        def entries(offsets, first, count):
+            return offsets[:, first // PER_COL : (first + count) // PER_COL]
+
+        def quantize(codes, scales, values):
+            nc.vector.quantize_mx(out=codes.bitcast(FP8X4), scales=scales, in_=values)
+
+        def product(acc, lhs_codes, lhs_scales, rhs_codes, rhs_scales, start, stop):
+            nc.tensor.matmul_mx(
+                out=acc,
+                lhsT=lhs_codes.bitcast(FP8X4),
+                lhsT_scale=lhs_scales,
+                rhs=rhs_codes.bitcast(FP8X4),
+                rhs_scale=rhs_scales,
+                start=start,
+                stop=stop,
+            )
+
+        key_list = lists.tile([P, I // PER_COL], U16, name="key_list")
+        note_list = lists.tile([P, I // PER_COL], U16, name="note_list")
+        place_list = lists.tile([P, I // PER_COL], U16, name="place_list")
+
+        q2_raw = sb.tile([P, PACK, Q], F32, name="q2_raw")
+        q_raw = sb.tile([P, PACK, Q], F32, name="q_raw")
+        note_planes = [sb.tile([P, U], F32, name=f"notes{t}") for t in range(PACK)]
+        key_words = sb.tile([P, T], I32, name="key_words")
+        key_bytes = sb.tile([P, T], U8, name="key_bytes")
+        msg_raw = [sb.tile([P, PACK, E // 2], F32, name=f"msg_raw{h}") for h in range(2)]
+        old_rows = [sb.tile([P, M], F32, name=f"old{a}") for a in range(E // P)]
+        windows = [sb.tile([P, M], F32, name=f"window{a}") for a in range(E // P)]
+        qs_cols = sb.tile([P, PACK], F32, name="qs_cols")
+        fade_cols = sb.tile([P, M // BANK, PACK], F32, name="fade_cols")
+        ident = sb.tile([P, P], F32, name="ident")
+
+        notes_by_plane = notes.rearrange("(p t) u -> p t u", t=PACK)
+        msgs_by_plane = msgs.rearrange("(p t) e -> p t e", t=PACK)
+        nc.sync.dma_start(note_list[:], offs2)
+        for t in range(PACK):
+            nc.sync.dma_start(out=note_planes[t][:], in_=notes_by_plane[:, t, :])
+        nc.sync.dma_start(key_list[:], offs)
+        nc.sync.dma_start(out=q2_raw[:], in_=query2.rearrange("(p t) q -> p t q", t=PACK))
+        nc.sync.dma_start(out=q_raw[:], in_=query.rearrange("(p t) q -> p t q", t=PACK))
+        nc.sync.dma_start(out=key_words[:], in_=keys_words[0].rearrange("p c t -> p (c t)").bitcast(I32))
+        nc.sync.dma_start(out=msg_raw[0][:], in_=msgs_by_plane[:, :, 0 : E // 2])
+        nc.sync.dma_start(place_list[:], offs3)
+        nc.sync.dma_start(out=msg_raw[1][:], in_=msgs_by_plane[:, :, E // 2 : E])
+        for a in range(E // P):
+            nc.sync.dma_start(out=old_rows[a][:], in_=old[a * P : (a + 1) * P, :])
+
+        nc.vector.memset(key_bytes[:].bitcast(I32), 0)
+        for quad in range(4):
+            nc.scalar.dma_start(
+                out=key_bytes[32 * quad : 32 * quad + 4, :].bitcast(I32),
+                in_=keys_scales[0, 4 * quad : 4 * quad + 4, :].bitcast(I32),
+            )
+        nc.scalar.dma_start(out=qs_cols[:], in_=qs.rearrange("(p t) o -> p (t o)", t=PACK))
+        nc.scalar.dma_start(out=fade_cols[:], in_=fade.rearrange("o (h p j) -> p (o h) j", j=PACK, p=P))
+        make_identity(nc, ident[:])
+        for a in range(E // P):
+            nc.vector.memset(windows[a][:], 0.0)
+
+        note_picked = sb.tile([P, PACK, I], BF16, name="note_picked")
+        for t in range(PACK):
+            window = note_planes[t][:].indirect(note_list[:])
+            if t % 2 == 0:
+                nc.scalar.activation(note_picked[:, t, :], window, COPY)
+            else:
+                nc.vector.tensor_copy(note_picked[:, t, :], window)
+        key_scales = sb.tile([P, I], U8, name="key_scales", align_bytes=64)
+        nc.vector.tensor_copy(key_scales[:], key_bytes[:].indirect(key_list[:]))
+        note_il = sb.tile([P, PACK * I], BF16, name="note_il", align_bytes=64)
+        note_codes = sb.tile([P, I], U32, name="note_codes", align_bytes=64)
+        note_scales = sb.tile([P, I], U8, name="note_scales", align_bytes=64)
+        nc.vector.tensor_copy(
+            out=note_il[:].rearrange("p (c i t) -> p c t i", i=4, t=PACK),
+            in_=note_picked[:].rearrange("p t (c i) -> p c t i", i=4),
+        )
+        quantize(note_codes[:], note_scales[:], note_il[:])
+
+        def prepare_queries(raw, name):
+            codes = sb.tile([P, Q], U32, name=name + "_codes", align_bytes=64)
+            scales = sb.tile([P, Q], U8, name=name + "_scales", align_bytes=64)
+            halves = [sb.tile([P, PACK * Q // 2], BF16, name=f"{name}_il{h}", align_bytes=64) for h in range(2)]
+            dealt = raw[:].rearrange("p t (s r) -> p s t r", r=PACK)
+            nc.vector.tensor_copy(out=halves[0][:].rearrange("p (r s t) -> p s t r", r=2, t=PACK), in_=dealt[:, :, :, 0:2])
+            nc.scalar.copy(out=halves[1][:].rearrange("p (r s t) -> p s t r", r=2, t=PACK), in_=dealt[:, :, :, 2:4])
+            for h in range(2):
+                cols = slice(h * Q // 2, (h + 1) * Q // 2)
+                quantize(codes[:, cols], scales[:, cols], halves[h][:])
+            return codes, scales
+
+        q2_codes, q2_scales = prepare_queries(q2_raw, "q2")
+        q_codes, q_scales = prepare_queries(q_raw, "q")
+
+        fade_banks = [ps_fade.tile([P, PACK, P], F32, name=f"fade_bank{h}") for h in range(M // BANK)]
+        for h in range(M // BANK):
+            for j in range(PACK):
+                nc.tensor.transpose(fade_banks[h][:, j, :], fade_cols[:, h, j : j + 1].to_broadcast([P, P]), ident[:])
+
+        scores = [ps.tile([P, PACK, CHUNK], F32, name=f"scores{c}", tag="acc") for c in range(CHUNKS)]
+        for c in range(CHUNKS):
+            slots = slice(c * CHUNK, (c + 1) * CHUNK)
+            for r in range(PACK):
+                rows = slice(r * P, (r + 1) * P)
+                product(scores[c][:, r, :], q2_codes[:, rows], q2_scales[:, rows], note_codes[:, slots], note_scales[:, slots], r == 0, False)
+        key_codes = sb.tile([P, I], U32, name="key_codes", align_bytes=64)
+        weights = [sb.tile([P, CHUNK, PACK], F32, name=f"weights{c}") for c in range(CHUNKS)]
+        for c in range(CHUNKS):
+            slots = slice(c * CHUNK, (c + 1) * CHUNK)
+            nc.vector.tensor_copy(key_codes[:, slots], key_words[:].bitcast(U32).indirect(entries(key_list, c * CHUNK, CHUNK)))
+            for r in range(PACK):
+                rows = slice(r * P, (r + 1) * P)
+                product(scores[c][:, r, :], q_codes[:, rows], q_scales[:, rows], key_codes[:, slots], key_scales[:, slots], False, r == PACK - 1)
+            nc.scalar.activation(weights[c][:], scores[c][:].rearrange("p r i -> p i r"), SIGMOID)
+
+        msg_il = [sb.tile([P, PACK * E // 2], BF16, name=f"msg_il{h}", align_bytes=64) for h in range(2)]
+        msg_codes = [sb.tile([P, E // 2], U32, name=f"msg_codes{h}", align_bytes=64) for h in range(2)]
+        msg_scales = [sb.tile([P, E // 2], U8, name=f"msg_scales{h}", align_bytes=64) for h in range(2)]
+
+        def interleave_messages(h):
+            nc.vector.tensor_copy(
+                out=msg_il[h][:].rearrange("p (c i t) -> p c t i", i=4, t=PACK),
+                in_=msg_raw[h][:].rearrange("p t (c i) -> p c t i", i=4),
+            )
+
+        def quantize_messages(h):
+            quantize(msg_codes[h][:], msg_scales[h][:], msg_il[h][:])
+
+        wq_il = [sb.tile([P, CHUNK * PACK], BF16, name=f"wq_il{c}", align_bytes=64) for c in range(CHUNKS)]
+        wq_codes = sb.tile([P, I], U32, name="wq_codes", align_bytes=64)
+        wq_scales = sb.tile([P, I], U8, name="wq_scales", align_bytes=64)
+        sums = sb.tile([P, E // P, I], F32, name="sums")
+        qs_spread = qs_cols[:].unsqueeze(1).to_broadcast([P, CHUNK, PACK])
+
+        def scatter(engine, a, first, count):
+            target = windows[a][:].indirect(entries(place_list, first, count))
+            if engine == "scalar":
+                nc.scalar.activation(target, sums[:, a, first : first + count], COPY)
+            else:
+                nc.vector.tensor_copy(target, sums[:, a, first : first + count])
+
+        def weigh(c):
+            nc.vector.tensor_tensor(wq_il[c][:].rearrange("p (i t) -> p i t", t=PACK), weights[c][:], qs_spread, MULT)
+
+        def deliver_early(c):
+            slots = slice(c * CHUNK, (c + 1) * CHUNK)
+            quantize(wq_codes[:, slots], wq_scales[:, slots], wq_il[c][:])
+            acc = ps.tile([P, 2, CHUNK], F32, name=f"early{c}", tag="acc")
+            for a in range(2):
+                cols = slice(a * P, (a + 1) * P)
+                product(acc[:, a, :], msg_codes[0][:, cols], msg_scales[0][:, cols], wq_codes[:, slots], wq_scales[:, slots], True, True)
+            nc.scalar.copy(out=sums[:, 0:2, slots], in_=acc[:])
+            scatter("scalar", 0, c * CHUNK, CHUNK)
+
+        interleave_messages(0)
+        weigh(0)
+        quantize_messages(0)
+        deliver_early(0)
+        weigh(1)
+        weigh(2)
+        deliver_early(1)
+        weigh(3)
+        deliver_early(2)
+        interleave_messages(1)
+        deliver_early(3)
+        quantize_messages(1)
+        for a in (3, 2):
+            cols = slice((a - 2) * P, (a - 1) * P)
+            acc = ps.tile([P, I], F32, name=f"late{a}", tag="acc")
+            product(acc[:], msg_codes[1][:, cols], msg_scales[1][:, cols], wq_codes[:], wq_scales[:], True, True)
+            if a == 3:
+                nc.vector.tensor_copy(out=sums[:, a, :], in_=acc[:])
+            else:
+                nc.scalar.copy(out=sums[:, a, :], in_=acc[:])
+
+        scatter("vector", 3, 0, I // 2)
+        for h in range(2):
+            scatter("scalar", 1, h * I // 2, I // 2)
+        for h in range(2):
+            scatter("scalar", 2, h * I // 2, I // 2)
+        scatter("scalar", 3, I // 2, I // 2)
+
+        for a in range(E // P):
+            for h in range(M // BANK):
+                part = old_rows[a][:, h * BANK : (h + 1) * BANK].rearrange("p (s j) -> p s j", j=PACK)
+                nc.vector.tensor_tensor(part, part, fade_banks[h][:].rearrange("p j s -> p s j"), MULT)
+
+        for a in range(E // P):
+            for h in range(M // BANK):
+                cols = slice(h * BANK, (h + 1) * BANK)
+                nc.vector.tensor_tensor(old_rows[a][:, cols], old_rows[a][:, cols], windows[a][:, cols], ADD)
+                nc.sync.dma_start(out=out[a * P : (a + 1) * P, cols], in_=old_rows[a][:, cols])

@@ -129,10 +129,10 @@ def tile_attend_twosources_delivered_lean_kernel(
         q2_codes, q2_scales = prepare_queries(q2_raw, "q2")
         q_codes, q_scales = prepare_queries(q_raw, "q")
 
-        fade_banks = [ps_fade.tile([P, PACK, P], F32, name=f"fade_bank{h}") for h in range(M // BANK)]
+        fade_banks = [ps_fade.tile([P, BANK], F32, name=f"fade_bank{h}") for h in range(M // BANK)]
         for h in range(M // BANK):
             for j in range(PACK):
-                nc.tensor.transpose(fade_banks[h][:, j, :], fade_cols[:, h, j : j + 1].to_broadcast([P, P]), ident[:])
+                nc.tensor.transpose(fade_banks[h][:, j::PACK], fade_cols[:, h, j : j + 1].to_broadcast([P, P]), ident[:])
 
         scores = [ps.tile([P, PACK, CHUNK], F32, name=f"scores{c}", tag="acc") for c in range(CHUNKS)]
         for c in range(CHUNKS):
@@ -201,29 +201,31 @@ def tile_attend_twosources_delivered_lean_kernel(
         interleave_messages(1)
         deliver_early(3)
         quantize_messages(1)
-        for a in (3, 2):
+        for a in (2, 3):
             cols = slice((a - 2) * P, (a - 1) * P)
             acc = ps.tile([P, I], F32, name=f"late{a}", tag="acc")
             product(acc[:], msg_codes[1][:, cols], msg_scales[1][:, cols], wq_codes[:], wq_scales[:], True, True)
-            if a == 3:
-                nc.vector.tensor_copy(out=sums[:, a, :], in_=acc[:])
-            else:
-                nc.scalar.copy(out=sums[:, a, :], in_=acc[:])
+            nc.scalar.copy(out=sums[:, a, :], in_=acc[:])
+            for h in range(2):
+                scatter("scalar", a, h * I // 2, I // 2)
 
-        scatter("vector", 3, 0, I // 2)
-        for h in range(2):
-            scatter("scalar", 1, h * I // 2, I // 2)
-        for h in range(2):
-            scatter("scalar", 2, h * I // 2, I // 2)
-        scatter("scalar", 3, I // 2, I // 2)
-
-        for a in range(E // P):
+        def fade_old(a):
             for h in range(M // BANK):
-                part = old_rows[a][:, h * BANK : (h + 1) * BANK].rearrange("p (s j) -> p s j", j=PACK)
-                nc.vector.tensor_tensor(part, part, fade_banks[h][:].rearrange("p j s -> p s j"), MULT)
+                part = old_rows[a][:, h * BANK : (h + 1) * BANK]
+                nc.vector.tensor_tensor(part, part, fade_banks[h][:], MULT)
 
-        for a in range(E // P):
-            for h in range(M // BANK):
-                cols = slice(h * BANK, (h + 1) * BANK)
-                nc.vector.tensor_tensor(old_rows[a][:, cols], old_rows[a][:, cols], windows[a][:, cols], ADD)
+        def finish(engine, a, pieces):
+            for h in range(pieces):
+                cols = slice(h * M // pieces, (h + 1) * M // pieces)
+                engine.tensor_tensor(old_rows[a][:, cols], old_rows[a][:, cols], windows[a][:, cols], ADD)
                 nc.sync.dma_start(out=out[a * P : (a + 1) * P, cols], in_=old_rows[a][:, cols])
+
+        fade_old(0)
+        fade_old(2)
+        scatter("vector", 1, 0, I)
+        fade_old(1)
+        fade_old(3)
+        finish(nc.gpsimd, 0, 1)
+        finish(nc.gpsimd, 2, 1)
+        finish(nc.vector, 1, 2)
+        finish(nc.vector, 3, 4)

@@ -66,32 +66,33 @@ def tile_attend_twosources_delivered_lean_kernel(
         old_rows = [sb.tile([P, M], F32, name=f"old{a}") for a in range(E // P)]
         windows = [sb.tile([P, M], F32, name=f"window{a}") for a in range(E // P)]
         qs_cols = sb.tile([P, PACK], F32, name="qs_cols")
-        fade_cols = sb.tile([P, M // BANK, PACK], F32, name="fade_cols")
+        fade_rows = sb.tile([P, P], F32, name="fade_rows")
+        fade_cols = sb.tile([P, M // P], F32, name="fade_cols")
         ident = sb.tile([P, P], F32, name="ident")
 
         notes_by_plane = notes.rearrange("(p t) u -> p t u", t=PACK)
         msgs_by_plane = msgs.rearrange("(p t) e -> p t e", t=PACK)
+        nc.gpsimd.memset(key_bytes[:].bitcast(I32), 0)
+        nc.gpsimd.memset(fade_rows[:], 0.0)
+        nc.sync.dma_start(out=note_planes[0][:], in_=notes_by_plane[:, 0, :])
         nc.sync.dma_start(note_list[:], offs2)
-        for t in range(PACK):
-            nc.sync.dma_start(out=note_planes[t][:], in_=notes_by_plane[:, t, :])
+        nc.sync.dma_start(out=note_planes[1][:], in_=notes_by_plane[:, 1, :])
+        nc.sync.dma_start(out=note_planes[2][:], in_=notes_by_plane[:, 2, :])
         nc.sync.dma_start(key_list[:], offs)
+        for r in range(4):
+            nc.sync.dma_start(out=key_bytes[r:P:32, :].bitcast(I32), in_=keys_scales[0, r:16:4, :].bitcast(I32))
+        nc.sync.dma_start(out=note_planes[3][:], in_=notes_by_plane[:, 3, :])
+        nc.sync.dma_start(out=fade_rows[0 : M // P, :], in_=fade.rearrange("o (k p) -> (o k) p", p=P))
         nc.sync.dma_start(out=q2_raw[:], in_=query2.rearrange("(p t) q -> p t q", t=PACK))
         nc.sync.dma_start(out=q_raw[:], in_=query.rearrange("(p t) q -> p t q", t=PACK))
         nc.sync.dma_start(out=key_words[:], in_=keys_words[0].rearrange("p c t -> p (c t)").bitcast(I32))
+        nc.sync.dma_start(out=qs_cols[:], in_=qs.rearrange("(p t) o -> p (t o)", t=PACK))
         nc.sync.dma_start(out=msg_raw[0][:], in_=msgs_by_plane[:, :, 0 : E // 2])
         nc.sync.dma_start(place_list[:], offs3)
         nc.sync.dma_start(out=msg_raw[1][:], in_=msgs_by_plane[:, :, E // 2 : E])
-        for a in range(E // P):
+        for a in (0, 3, 1, 2):
             nc.sync.dma_start(out=old_rows[a][:], in_=old[a * P : (a + 1) * P, :])
 
-        nc.vector.memset(key_bytes[:].bitcast(I32), 0)
-        for quad in range(4):
-            nc.scalar.dma_start(
-                out=key_bytes[32 * quad : 32 * quad + 4, :].bitcast(I32),
-                in_=keys_scales[0, 4 * quad : 4 * quad + 4, :].bitcast(I32),
-            )
-        nc.scalar.dma_start(out=qs_cols[:], in_=qs.rearrange("(p t) o -> p (t o)", t=PACK))
-        nc.scalar.dma_start(out=fade_cols[:], in_=fade.rearrange("o (h p j) -> p (o h) j", j=PACK, p=P))
         make_identity(nc, ident[:])
         for a in range(E // P):
             nc.vector.memset(windows[a][:], 0.0)
@@ -114,48 +115,37 @@ def tile_attend_twosources_delivered_lean_kernel(
         )
         quantize(note_codes[:], note_scales[:], note_il[:])
 
-        def prepare_queries(raw, name):
-            codes = sb.tile([P, Q], U32, name=name + "_codes", align_bytes=64)
-            scales = sb.tile([P, Q], U8, name=name + "_scales", align_bytes=64)
-            halves = [sb.tile([P, PACK * Q // 2], BF16, name=f"{name}_il{h}", align_bytes=64) for h in range(2)]
-            dealt = raw[:].rearrange("p t (s r) -> p s t r", r=PACK)
-            nc.vector.tensor_copy(out=halves[0][:].rearrange("p (r s t) -> p s t r", r=2, t=PACK), in_=dealt[:, :, :, 0:2])
-            nc.scalar.copy(out=halves[1][:].rearrange("p (r s t) -> p s t r", r=2, t=PACK), in_=dealt[:, :, :, 2:4])
-            for h in range(2):
-                cols = slice(h * Q // 2, (h + 1) * Q // 2)
-                quantize(codes[:, cols], scales[:, cols], halves[h][:])
-            return codes, scales
-
-        q2_codes, q2_scales = prepare_queries(q2_raw, "q2")
-        q_codes, q_scales = prepare_queries(q_raw, "q")
+        q2_il = sb.tile([P, PACK * Q], BF16, name="q2_il", align_bytes=64)
+        q2_codes = sb.tile([P, Q], U32, name="q2_codes", align_bytes=64)
+        q2_scales = sb.tile([P, Q], U8, name="q2_scales", align_bytes=64)
+        nc.scalar.copy(
+            out=q2_il[:].rearrange("p (r s t) -> p s t r", r=PACK, t=PACK),
+            in_=q2_raw[:].rearrange("p t (s r) -> p s t r", r=PACK),
+        )
+        q_il = [sb.tile([P, PACK * Q // 2], BF16, name=f"q_il{h}", align_bytes=64) for h in range(2)]
+        q_codes = sb.tile([P, Q], U32, name="q_codes", align_bytes=64)
+        q_scales = sb.tile([P, Q], U8, name="q_scales", align_bytes=64)
+        q_dealt = q_raw[:].rearrange("p t (s r) -> p s t r", r=PACK)
+        nc.vector.tensor_copy(out=q_il[0][:].rearrange("p (r s t) -> p s t r", r=2, t=PACK), in_=q_dealt[:, :, :, 0:2])
+        nc.scalar.copy(out=q_il[1][:].rearrange("p (r s t) -> p s t r", r=2, t=PACK), in_=q_dealt[:, :, :, 2:4])
+        quantize(q2_codes[:], q2_scales[:], q2_il[:])
+        for h in range(2):
+            cols = slice(h * Q // 2, (h + 1) * Q // 2)
+            quantize(q_codes[:, cols], q_scales[:, cols], q_il[h][:])
 
         fade_banks = [ps_fade.tile([P, BANK], F32, name=f"fade_bank{h}") for h in range(M // BANK)]
-        for h in range(M // BANK):
-            for j in range(PACK):
-                nc.tensor.transpose(fade_banks[h][:, j::PACK], fade_cols[:, h, j : j + 1].to_broadcast([P, P]), ident[:])
-
-        scores = [ps.tile([P, PACK, CHUNK], F32, name=f"scores{c}", tag="acc") for c in range(CHUNKS)]
-        for c in range(CHUNKS):
-            slots = slice(c * CHUNK, (c + 1) * CHUNK)
-            for r in range(PACK):
-                rows = slice(r * P, (r + 1) * P)
-                product(scores[c][:, r, :], q2_codes[:, rows], q2_scales[:, rows], note_codes[:, slots], note_scales[:, slots], r == 0, False)
-        key_codes = sb.tile([P, I], U32, name="key_codes", align_bytes=64)
-        weights = [sb.tile([P, CHUNK, PACK], F32, name=f"weights{c}") for c in range(CHUNKS)]
-        for c in range(CHUNKS):
-            slots = slice(c * CHUNK, (c + 1) * CHUNK)
-            nc.vector.tensor_copy(key_codes[:, slots], key_words[:].bitcast(U32).indirect(entries(key_list, c * CHUNK, CHUNK)))
-            for r in range(PACK):
-                rows = slice(r * P, (r + 1) * P)
-                product(scores[c][:, r, :], q_codes[:, rows], q_scales[:, rows], key_codes[:, slots], key_scales[:, slots], False, r == PACK - 1)
-            nc.scalar.activation(weights[c][:], scores[c][:].rearrange("p r i -> p i r"), SIGMOID)
+        nc.tensor.transpose(fade_banks[1][:, 0:P], fade_rows[:], ident[:])
+        nc.vector.tensor_copy(out=fade_cols[:], in_=fade_banks[1][:, 0 : M // P])
+        for k in range(M // P):
+            h, j = divmod(k, BANK // P)
+            nc.tensor.transpose(fade_banks[h][:, j * P : (j + 1) * P], fade_cols[:, k : k + 1].to_broadcast([P, P]), ident[:])
 
         msg_il = [sb.tile([P, PACK * E // 2], BF16, name=f"msg_il{h}", align_bytes=64) for h in range(2)]
         msg_codes = [sb.tile([P, E // 2], U32, name=f"msg_codes{h}", align_bytes=64) for h in range(2)]
         msg_scales = [sb.tile([P, E // 2], U8, name=f"msg_scales{h}", align_bytes=64) for h in range(2)]
 
-        def interleave_messages(h):
-            nc.vector.tensor_copy(
+        def interleave_messages(h, copy):
+            copy(
                 out=msg_il[h][:].rearrange("p (c i t) -> p c t i", i=4, t=PACK),
                 in_=msg_raw[h][:].rearrange("p t (c i) -> p c t i", i=4),
             )
@@ -163,18 +153,34 @@ def tile_attend_twosources_delivered_lean_kernel(
         def quantize_messages(h):
             quantize(msg_codes[h][:], msg_scales[h][:], msg_il[h][:])
 
+        interleave_messages(0, nc.scalar.copy)
+
+        scores = [ps.tile([P, PACK, CHUNK], F32, name=f"scores{c}", tag="acc") for c in range(CHUNKS)]
+        key_codes = sb.tile([P, I], U32, name="key_codes", align_bytes=64)
+        weights = [sb.tile([P, CHUNK, PACK], F32, name=f"weights{c}") for c in range(CHUNKS)]
+        for c in range(CHUNKS):
+            slots = slice(c * CHUNK, (c + 1) * CHUNK)
+            for r in range(PACK):
+                rows = slice(r * P, (r + 1) * P)
+                product(scores[c][:, r, :], q2_codes[:, rows], q2_scales[:, rows], note_codes[:, slots], note_scales[:, slots], r == 0, False)
+            nc.vector.tensor_copy(key_codes[:, slots], key_words[:].bitcast(U32).indirect(entries(key_list, c * CHUNK, CHUNK)))
+            for r in range(PACK):
+                rows = slice(r * P, (r + 1) * P)
+                product(scores[c][:, r, :], q_codes[:, rows], q_scales[:, rows], key_codes[:, slots], key_scales[:, slots], False, r == PACK - 1)
+            nc.scalar.activation(weights[c][:], scores[c][:].rearrange("p r i -> p i r"), SIGMOID)
+
         wq_il = [sb.tile([P, CHUNK * PACK], BF16, name=f"wq_il{c}", align_bytes=64) for c in range(CHUNKS)]
         wq_codes = sb.tile([P, I], U32, name="wq_codes", align_bytes=64)
         wq_scales = sb.tile([P, I], U8, name="wq_scales", align_bytes=64)
-        sums = sb.tile([P, E // P, I], F32, name="sums")
+        sums = sb.tile([P, 2, I], F32, name="sums")
         qs_spread = qs_cols[:].unsqueeze(1).to_broadcast([P, CHUNK, PACK])
 
-        def scatter(engine, a, first, count):
+        def scatter(engine, a, source, first, count):
             target = windows[a][:].indirect(entries(place_list, first, count))
             if engine == "scalar":
-                nc.scalar.activation(target, sums[:, a, first : first + count], COPY)
+                nc.scalar.activation(target, source[:, first : first + count], COPY)
             else:
-                nc.vector.tensor_copy(target, sums[:, a, first : first + count])
+                nc.vector.tensor_copy(target, source[:, first : first + count])
 
         def weigh(c):
             nc.vector.tensor_tensor(wq_il[c][:].rearrange("p (i t) -> p i t", t=PACK), weights[c][:], qs_spread, MULT)
@@ -186,10 +192,9 @@ def tile_attend_twosources_delivered_lean_kernel(
             for a in range(2):
                 cols = slice(a * P, (a + 1) * P)
                 product(acc[:, a, :], msg_codes[0][:, cols], msg_scales[0][:, cols], wq_codes[:, slots], wq_scales[:, slots], True, True)
-            nc.scalar.copy(out=sums[:, 0:2, slots], in_=acc[:])
-            scatter("scalar", 0, c * CHUNK, CHUNK)
+            nc.scalar.copy(out=sums[:, :, slots], in_=acc[:])
+            scatter("scalar", 0, sums[:, 0, :], c * CHUNK, CHUNK)
 
-        interleave_messages(0)
         weigh(0)
         quantize_messages(0)
         deliver_early(0)
@@ -198,16 +203,24 @@ def tile_attend_twosources_delivered_lean_kernel(
         deliver_early(1)
         weigh(3)
         deliver_early(2)
-        interleave_messages(1)
+        interleave_messages(1, nc.vector.tensor_copy)
         deliver_early(3)
         quantize_messages(1)
-        for a in (2, 3):
+        scatter("scalar", 1, sums[:, 1, :], CHUNK, I - CHUNK)
+        scatter("scalar", 1, sums[:, 1, :], 0, CHUNK)
+
+        late_sums = {}
+
+        def deliver_late(a, copy):
             cols = slice((a - 2) * P, (a - 1) * P)
             acc = ps.tile([P, I], F32, name=f"late{a}", tag="acc")
             product(acc[:], msg_codes[1][:, cols], msg_scales[1][:, cols], wq_codes[:], wq_scales[:], True, True)
-            nc.scalar.copy(out=sums[:, a, :], in_=acc[:])
-            for h in range(2):
-                scatter("scalar", a, h * I // 2, I // 2)
+            late_sums[a] = sb.tile([P, I], F32, name=f"late_sums{a}")
+            copy(out=late_sums[a][:], in_=acc[:])
+
+        deliver_late(2, nc.scalar.copy)
+        scatter("scalar", 2, late_sums[2][:], 0, CHUNK)
+        scatter("scalar", 2, late_sums[2][:], CHUNK, I - CHUNK)
 
         def fade_old(a):
             for h in range(M // BANK):
@@ -221,11 +234,12 @@ def tile_attend_twosources_delivered_lean_kernel(
                 nc.sync.dma_start(out=out[a * P : (a + 1) * P, cols], in_=old_rows[a][:, cols])
 
         fade_old(0)
-        fade_old(2)
-        scatter("vector", 1, 0, I)
-        fade_old(1)
+        deliver_late(3, nc.vector.tensor_copy)
         fade_old(3)
+        scatter("vector", 3, late_sums[3][:], 0, I)
+        fade_old(1)
+        fade_old(2)
         finish(nc.gpsimd, 0, 1)
-        finish(nc.gpsimd, 2, 1)
+        finish(nc.gpsimd, 3, 1)
         finish(nc.vector, 1, 2)
-        finish(nc.vector, 3, 4)
+        finish(nc.vector, 2, 4)

from contextlib import ExitStack

import concourse.mybir as mybir
from concourse.masks import make_identity

D, T, I, Q, E, U, M = 512, 2048, 512, 512, 512, 1024, 1024
FLOPS = 2 * Q * I * D * 2 + 2 * E * I * Q

F32 = mybir.dt.float32
BF16 = mybir.dt.bfloat16
I32 = mybir.dt.int32
U32 = mybir.dt.uint32
U16 = mybir.dt.uint16
U8 = mybir.dt.uint8
FP8X4 = mybir.dt.float8_e4m3fn_x4
MULT = mybir.AluOpType.mult
ADD = mybir.AluOpType.add
COPY = mybir.ActivationFunctionType.Copy
SIGMOID = mybir.ActivationFunctionType.Sigmoid

P = 128
PACK = 4
CHUNK = 128
CHUNKS = I // CHUNK
PER_COL = 16
BANK = 512


def tile_attend_twosources_delivered_lean_kernel(
    tc, query, query2, keys_words, keys_scales, notes, qs, msgs, old, fade, offs, offs2, offs3, out
):
    nc = tc.nc
    with ExitStack() as ctx:
        lists = ctx.enter_context(tc.tile_pool(name="lists", bufs=1))
        sb = ctx.enter_context(tc.tile_pool(name="sb", bufs=1))
        ps_fade = ctx.enter_context(tc.psum_pool(name="ps_fade", bufs=1))
        ps = ctx.enter_context(tc.psum_pool(name="ps", bufs=6))

        def entries(offsets, first, count):
            return offsets[:, first // PER_COL : (first + count) // PER_COL]

        def quantize(codes, scales, values):
            nc.vector.quantize_mx(out=codes.bitcast(FP8X4), scales=scales, in_=values)

        def product(acc, lhs_codes, lhs_scales, rhs_codes, rhs_scales, start, stop):
            nc.tensor.matmul_mx(
                out=acc,
                lhsT=lhs_codes.bitcast(FP8X4),
                lhsT_scale=lhs_scales,
                rhs=rhs_codes.bitcast(FP8X4),
                rhs_scale=rhs_scales,
                start=start,
                stop=stop,
            )

        key_list = lists.tile([P, I // PER_COL], U16, name="key_list")
        note_list = lists.tile([P, I // PER_COL], U16, name="note_list")
        place_list = lists.tile([P, I // PER_COL], U16, name="place_list")

        q2_raw = sb.tile([P, PACK, Q], F32, name="q2_raw")
        q_raw = sb.tile([P, PACK, Q], F32, name="q_raw")
        note_planes = [sb.tile([P, U], F32, name=f"notes{t}") for t in range(PACK)]
        key_words = sb.tile([P, T], I32, name="key_words")
        key_bytes = sb.tile([P, T], U8, name="key_bytes")
        msg_raw = [sb.tile([P, PACK, E // 2], F32, name=f"msg_raw{h}") for h in range(2)]
        old_rows = [sb.tile([P, M], F32, name=f"old{a}") for a in range(E // P)]
        windows = [sb.tile([P, M], F32, name=f"window{a}") for a in range(E // P)]
        qs_cols = sb.tile([P, PACK], F32, name="qs_cols")
        fade_rows = sb.tile([P, P], F32, name="fade_rows")
        fade_cols = sb.tile([P, M // P], F32, name="fade_cols")
        ident = sb.tile([P, P], F32, name="ident")

        notes_by_plane = notes.rearrange("(p t) u -> p t u", t=PACK)
        msgs_by_plane = msgs.rearrange("(p t) e -> p t e", t=PACK)
        nc.gpsimd.memset(key_bytes[:].bitcast(I32), 0)
        nc.gpsimd.memset(fade_rows[:], 0.0)
        nc.sync.dma_start(out=note_planes[0][:], in_=notes_by_plane[:, 0, :])
        nc.sync.dma_start(note_list[:], offs2)
        nc.sync.dma_start(out=note_planes[1][:], in_=notes_by_plane[:, 1, :])
        nc.sync.dma_start(out=note_planes[2][:], in_=notes_by_plane[:, 2, :])
        nc.sync.dma_start(key_list[:], offs)
        for r in range(4):
            nc.sync.dma_start(out=key_bytes[r:P:32, :].bitcast(I32), in_=keys_scales[0, r:16:4, :].bitcast(I32))
        nc.sync.dma_start(out=note_planes[3][:], in_=notes_by_plane[:, 3, :])
        nc.sync.dma_start(out=fade_rows[0 : M // P, :], in_=fade.rearrange("o (k p) -> (o k) p", p=P))
        nc.sync.dma_start(out=q2_raw[:], in_=query2.rearrange("(p t) q -> p t q", t=PACK))
        nc.sync.dma_start(out=q_raw[:], in_=query.rearrange("(p t) q -> p t q", t=PACK))
        nc.sync.dma_start(out=key_words[:], in_=keys_words[0].rearrange("p c t -> p (c t)").bitcast(I32))
        nc.sync.dma_start(out=qs_cols[:], in_=qs.rearrange("(p t) o -> p (t o)", t=PACK))
        nc.sync.dma_start(out=msg_raw[0][:], in_=msgs_by_plane[:, :, 0 : E // 2])
        nc.sync.dma_start(place_list[:], offs3)
        nc.sync.dma_start(out=msg_raw[1][:], in_=msgs_by_plane[:, :, E // 2 : E])
        for a in (0, 3, 1, 2):
            nc.sync.dma_start(out=old_rows[a][:], in_=old[a * P : (a + 1) * P, :])

        make_identity(nc, ident[:])
        for a in range(E // P):
            nc.vector.memset(windows[a][:], 0.0)

        note_picked = sb.tile([P, PACK, I], BF16, name="note_picked")
        for t in range(PACK):
            window = note_planes[t][:].indirect(note_list[:])
            if t % 2 == 0:
                nc.scalar.activation(note_picked[:, t, :], window, COPY)
            else:
                nc.vector.tensor_copy(note_picked[:, t, :], window)
        key_scales = sb.tile([P, I], U8, name="key_scales", align_bytes=64)
        nc.vector.tensor_copy(key_scales[:], key_bytes[:].indirect(key_list[:]))
        note_il = sb.tile([P, PACK * I], BF16, name="note_il", align_bytes=64)
        note_codes = sb.tile([P, I], U32, name="note_codes", align_bytes=64)
        note_scales = sb.tile([P, I], U8, name="note_scales", align_bytes=64)
        nc.vector.tensor_copy(
            out=note_il[:].rearrange("p (c i t) -> p c t i", i=4, t=PACK),
            in_=note_picked[:].rearrange("p t (c i) -> p c t i", i=4),
        )
        quantize(note_codes[:], note_scales[:], note_il[:])

        q2_il = sb.tile([P, PACK * Q], BF16, name="q2_il", align_bytes=64)
        q2_codes = sb.tile([P, Q], U32, name="q2_codes", align_bytes=64)
        q2_scales = sb.tile([P, Q], U8, name="q2_scales", align_bytes=64)
        nc.scalar.copy(
            out=q2_il[:].rearrange("p (r s t) -> p s t r", r=PACK, t=PACK),
            in_=q2_raw[:].rearrange("p t (s r) -> p s t r", r=PACK),
        )
        q_il = [sb.tile([P, PACK * Q // 2], BF16, name=f"q_il{h}", align_bytes=64) for h in range(2)]
        q_codes = sb.tile([P, Q], U32, name="q_codes", align_bytes=64)
        q_scales = sb.tile([P, Q], U8, name="q_scales", align_bytes=64)
        q_dealt = q_raw[:].rearrange("p t (s r) -> p s t r", r=PACK)
        nc.vector.tensor_copy(out=q_il[0][:].rearrange("p (r s t) -> p s t r", r=2, t=PACK), in_=q_dealt[:, :, :, 0:2])
        nc.scalar.copy(out=q_il[1][:].rearrange("p (r s t) -> p s t r", r=2, t=PACK), in_=q_dealt[:, :, :, 2:4])
        quantize(q2_codes[:], q2_scales[:], q2_il[:])
        for h in range(2):
            cols = slice(h * Q // 2, (h + 1) * Q // 2)
            quantize(q_codes[:, cols], q_scales[:, cols], q_il[h][:])

        fade_banks = [ps_fade.tile([P, BANK], F32, name=f"fade_bank{h}") for h in range(M // BANK)]
        nc.tensor.transpose(fade_banks[1][:, 0:P], fade_rows[:], ident[:])
        nc.vector.tensor_copy(out=fade_cols[:], in_=fade_banks[1][:, 0 : M // P])
        for k in range(M // P):
            h, j = divmod(k, BANK // P)
            nc.tensor.transpose(fade_banks[h][:, j * P : (j + 1) * P], fade_cols[:, k : k + 1].to_broadcast([P, P]), ident[:])

        msg_il = [sb.tile([P, PACK * E // 2], BF16, name=f"msg_il{h}", align_bytes=64) for h in range(2)]
        msg_codes = [sb.tile([P, E // 2], U32, name=f"msg_codes{h}", align_bytes=64) for h in range(2)]
        msg_scales = [sb.tile([P, E // 2], U8, name=f"msg_scales{h}", align_bytes=64) for h in range(2)]

        def interleave_messages(h, copy):
            copy(
                out=msg_il[h][:].rearrange("p (c i t) -> p c t i", i=4, t=PACK),
                in_=msg_raw[h][:].rearrange("p t (c i) -> p c t i", i=4),
            )

        def quantize_messages(h):
            quantize(msg_codes[h][:], msg_scales[h][:], msg_il[h][:])

        interleave_messages(0, nc.scalar.copy)

        scores = [ps.tile([P, PACK, CHUNK], F32, name=f"scores{c}", tag="acc") for c in range(CHUNKS)]
        key_codes = sb.tile([P, I], U32, name="key_codes", align_bytes=64)
        weights = [sb.tile([P, CHUNK, PACK], F32, name=f"weights{c}") for c in range(CHUNKS)]
        for c in range(CHUNKS):
            slots = slice(c * CHUNK, (c + 1) * CHUNK)
            for r in range(PACK):
                rows = slice(r * P, (r + 1) * P)
                product(scores[c][:, r, :], q2_codes[:, rows], q2_scales[:, rows], note_codes[:, slots], note_scales[:, slots], r == 0, False)
            nc.vector.tensor_copy(key_codes[:, slots], key_words[:].bitcast(U32).indirect(entries(key_list, c * CHUNK, CHUNK)))
            for r in range(PACK):
                rows = slice(r * P, (r + 1) * P)
                product(scores[c][:, r, :], q_codes[:, rows], q_scales[:, rows], key_codes[:, slots], key_scales[:, slots], False, r == PACK - 1)
            nc.scalar.activation(weights[c][:], scores[c][:].rearrange("p r i -> p i r"), SIGMOID)

        wq_il = [sb.tile([P, CHUNK * PACK], BF16, name=f"wq_il{c}", align_bytes=64) for c in range(CHUNKS)]
        wq_codes = sb.tile([P, I], U32, name="wq_codes", align_bytes=64)
        wq_scales = sb.tile([P, I], U8, name="wq_scales", align_bytes=64)
        sums = sb.tile([P, 2, I], F32, name="sums")
        qs_spread = qs_cols[:].unsqueeze(1).to_broadcast([P, CHUNK, PACK])

        def scatter(engine, a, source, first, count):
            target = windows[a][:].indirect(entries(place_list, first, count))
            if engine == "scalar":
                nc.scalar.activation(target, source[:, first : first + count], COPY)
            else:
                nc.vector.tensor_copy(target, source[:, first : first + count])

        def weigh(c):
            nc.vector.tensor_tensor(wq_il[c][:].rearrange("p (i t) -> p i t", t=PACK), weights[c][:], qs_spread, MULT)

        def deliver_early(c):
            slots = slice(c * CHUNK, (c + 1) * CHUNK)
            quantize(wq_codes[:, slots], wq_scales[:, slots], wq_il[c][:])
            acc = ps.tile([P, 2, CHUNK], F32, name=f"early{c}", tag="acc")
            for a in range(2):
                cols = slice(a * P, (a + 1) * P)
                product(acc[:, a, :], msg_codes[0][:, cols], msg_scales[0][:, cols], wq_codes[:, slots], wq_scales[:, slots], True, True)
            nc.scalar.copy(out=sums[:, :, slots], in_=acc[:])
            scatter("scalar", 0, sums[:, 0, :], c * CHUNK, CHUNK)

        weigh(0)
        quantize_messages(0)
        deliver_early(0)
        weigh(1)
        weigh(2)
        deliver_early(1)
        weigh(3)
        deliver_early(2)
        interleave_messages(1, nc.vector.tensor_copy)
        deliver_early(3)
        quantize_messages(1)
        scatter("scalar", 1, sums[:, 1, :], CHUNK, I - CHUNK)
        scatter("scalar", 1, sums[:, 1, :], 0, CHUNK)

        late_sums = {}

        def deliver_late(a, copy):
            cols = slice((a - 2) * P, (a - 1) * P)
            acc = ps.tile([P, I], F32, name=f"late{a}", tag="acc")
            product(acc[:], msg_codes[1][:, cols], msg_scales[1][:, cols], wq_codes[:], wq_scales[:], True, True)
            late_sums[a] = sb.tile([P, I], F32, name=f"late_sums{a}")
            copy(out=late_sums[a][:], in_=acc[:])

        deliver_late(2, nc.scalar.copy)
        scatter("scalar", 2, late_sums[2][:], 0, CHUNK)
        scatter("scalar", 2, late_sums[2][:], CHUNK, I - CHUNK)

        def fade_old(a):
            for h in range(M // BANK):
                part = old_rows[a][:, h * BANK : (h + 1) * BANK]
                nc.vector.tensor_tensor(part, part, fade_banks[h][:], MULT)

        def finish(engine, a, pieces):
            for h in range(pieces):
                cols = slice(h * M // pieces, (h + 1) * M // pieces)
                engine.tensor_tensor(old_rows[a][:, cols], old_rows[a][:, cols], windows[a][:, cols], ADD)
                nc.sync.dma_start(out=out[a * P : (a + 1) * P, cols], in_=old_rows[a][:, cols])

        fade_old(0)
        deliver_late(3, nc.vector.tensor_copy)
        fade_old(3)
        scatter("vector", 3, late_sums[3][:], 0, I)
        fade_old(1)
        fade_old(2)
        finish(nc.gpsimd, 0, 1)
        finish(nc.gpsimd, 3, 1)
        finish(nc.vector, 1, 2)
        finish(nc.vector, 2, 4)
